import numpy as np
import ml_dtypes


def mxq(x, axis, fmt="e4m3"):
    dtype, down = {"e4m3": (ml_dtypes.float8_e4m3fn, 7), "e5m2": (ml_dtypes.float8_e5m2, 14)}[fmt]
    v = np.moveaxis(np.asarray(x, np.float32).astype(ml_dtypes.bfloat16).astype(np.float64), axis, -1)
    blocks = v.reshape(v.shape[:-1] + (-1, 32))
    amax = np.abs(blocks).max(-1, keepdims=True)
    byte = np.maximum(np.where(amax > 0, np.frexp(amax)[1] - 1 + 127, 0) - down, 1)
    scale = np.exp2(byte - 127.0)
    codes = (blocks / scale).astype(np.float32).astype(dtype).astype(np.float64)
    return np.moveaxis((codes * scale).reshape(v.shape), -1, axis)


WIDE = False


def mx_kscale(k):
    if not WIDE:
        return np.ones(k)
    levels = np.array([10, -10, 5, -5, 0])
    if k % 512:
        return np.exp2(np.random.permutation(np.resize(levels, k // 32))).repeat(32)
    a = np.empty((k // 512, 16))
    for p in range(k // 512):
        a[p, :8] = np.random.permutation(np.resize(levels, 8))
        for g in range(8):
            far = levels[np.abs(levels - a[p, g]) >= 10]
            a[p, g + 8] = far[np.random.randint(len(far))]
    return np.exp2(a.ravel()).repeat(32)


def f64(x):
    return np.asarray(x).astype(np.float64)


def striped(idx):
    return np.tile(idx.reshape(-1, 16).T, (8, 1)).astype(np.uint16)


def unstriped(offs):
    return offs[:16].T.reshape(-1).astype(np.int64)


def striped8(idx):
    return np.concatenate([x.reshape(-1, 16).T for x in idx]).astype(np.uint16)


def runs(offs, k):
    lists = np.stack([offs[16 * r : 16 * r + 16].T.reshape(-1) for r in range(8)]).astype(np.int64)
    return lists[np.arange(k) % 512 // 64]


def pack_weight(w):
    k, n = w.shape
    w = f64(np.asarray(w, np.float32).astype(ml_dtypes.bfloat16)).reshape(k // 32, 32, n)
    amax = np.abs(w).max(1)
    byte = np.clip(np.where(amax > 0, np.frexp(amax)[1] - 1 + 127 - 7, 1), 1, 254)
    scaled = (w * np.exp2(127.0 - byte)[:, None, :]).reshape(k, n).astype(np.float32)
    words = np.ascontiguousarray(scaled.reshape(k // 512, 128, 4, n).transpose(0, 1, 3, 2)).astype(ml_dtypes.float8_e4m3fn).view(np.uint8)
    return words, np.ascontiguousarray(byte.astype(np.uint8).reshape(k // 512, 16, n))


def unpack_weight(words, scales):
    g, p, n, _ = words.shape
    vals = np.ascontiguousarray(words).view(ml_dtypes.float8_e4m3fn).astype(np.float64) * np.repeat(np.exp2(scales.astype(np.float64) - 127.0), 8, axis=1)[..., None]
    return vals.transpose(0, 1, 3, 2).reshape(g * 512, n)


K, T, S, N, W = 512, 2048, 512, 512, 256


def setup_inputs():
    n = np.random.standard_normal
    s = mx_kscale(K)[:, None]
    packed_xT = pack_weight(n((K, T)) * s)
    perm = np.stack([np.random.permutation(S) for _ in range(8)])
    return {
        "x_words": packed_xT[0],
        "x_scales": packed_xT[1],
        "w1": (n((K, N)) / np.sqrt(2 * K) / s).astype(np.float32),
        "w2": (n((K, N)) / np.sqrt(2 * K) / s).astype(np.float32),
        "offs": striped(np.random.permutation(T)[:S]),
        "hz": striped8(np.random.randint(0, T, (8, S))),
        "n1": striped8(perm[:, :W]),
        "n2": striped8(perm[:, W:]),
    }


def reference(x_words, x_scales, w1, w2, offs, hz, n1, n2):
    xq = unpack_weight(x_words, x_scales)[:, unstriped(offs)]
    x_hz = unpack_weight(x_words, x_scales)[np.arange(K)[:, None], runs(hz, K)]
    h = mxq(f64(w1), 0, "e4m3").T @ xq + mxq(f64(w2), 0, "e4m3").T @ x_hz
    pa = h[np.arange(N)[:, None], runs(n1, N)]
    pb = h[np.arange(N)[:, None], runs(n2, N)]
    rb = np.maximum(pa, pb)
    ra = pa / (np.abs(pb) + 0.5)
    ds = np.zeros((N, S))
    ds[np.arange(N)[:, None], runs(n1, N)] = ra
    out = ds.copy()
    out[np.arange(N)[:, None], runs(n2, N)] = rb
    return out

@@ -1,0 +1,125 @@
+from contextlib import ExitStack
+
+import concourse.mybir as mybir
+
+K, T, S, N, W = 512, 2048, 512, 512, 256
+FLOPS = 2 * 2 * K * S * N
+
+F32 = mybir.dt.float32
+BF16 = mybir.dt.bfloat16
+I32 = mybir.dt.int32
+U32 = mybir.dt.uint32
+U16 = mybir.dt.uint16
+U8 = mybir.dt.uint8
+FP8X4 = mybir.dt.float8_e4m3fn_x4
+ACT = mybir.ActivationFunctionType
+ALU = mybir.AluOpType
+
+P = 128
+PACK = 4
+TILES = N // P
+
+
+def tile_picked_othratio_none_p_kernel(tc, x_words, x_scales, w1, w2, offs, hz, n1, n2, out):
+    nc = tc.nc
+    with ExitStack() as ctx:
+        keep = ctx.enter_context(tc.tile_pool(name="keep", bufs=1))
+        psum = ctx.enter_context(tc.psum_pool(name="psum", bufs=1))
+
+        words = keep.tile([P, T], I32, name="words", align_bytes=64)
+        scales = keep.tile([P, T], U8, name="scales", align_bytes=64)
+        offs_t = keep.tile([P, S // 16], U16, name="offs_t")
+        hz_t = keep.tile([P, S // 16], U16, name="hz_t")
+        n1_t = keep.tile([P, W // 16], U16, name="n1_t")
+        n2_t = keep.tile([P, W // 16], U16, name="n2_t")
+        raw1 = keep.tile([P, PACK, N], F32, name="raw1", align_bytes=64)
+        raw2 = keep.tile([P, PACK, N], F32, name="raw2", align_bytes=64)
+        half = keep.tile([P, 1], F32, name="half")
+
+        picked_bytes = keep.tile([P, 2 * S], U8, name="picked_bytes", align_bytes=64)
+        planes = keep.tile([P, 2 * S], U8, name="planes", align_bytes=64)
+        offs_words = keep.tile([P, S], U32, name="offs_words", align_bytes=64)
+        hz_words = keep.tile([P, S], U32, name="hz_words", align_bytes=64)
+
+        nc.gpsimd.memset(planes[:].bitcast(I32), 0)
+        nc.gpsimd.memset(half[:], 0.5)
+
+        nc.sync.dma_start(hz_t[:], hz)
+        nc.sync.dma_start(offs_t[:], offs)
+        scale_rows = x_scales[0].bitcast(I32)
+        nc.sync.dma_start(scales[:].bitcast(I32), scale_rows.unsqueeze(1).to_broadcast([16, 8, T // 4]))
+        nc.sync.dma_start(n1_t[:], n1)
+        nc.sync.dma_start(words[:], x_words[0].rearrange("p c r -> p (c r)").bitcast(I32))
+        nc.sync.dma_start(raw1[:], w1.rearrange("(p j) m -> p j m", j=PACK))
+        nc.sync.dma_start(raw2[:], w2.rearrange("(p j) m -> p j m", j=PACK))
+        nc.sync.dma_start(n2_t[:], n2)
+
+        nc.vector.tensor_copy(picked_bytes[:, :S], scales[:].indirect(offs_t[:]))
+        nc.vector.tensor_copy(picked_bytes[:, S:], scales[:].indirect(hz_t[:]))
+        for i in range(4):
+            nc.scalar.dma_start(planes[:].bitcast(I32)[i:P:32, :], picked_bytes[:].bitcast(I32)[8 * i : P : 32, :])
+        nc.vector.tensor_copy(offs_words[:], words[:].bitcast(U32).indirect(offs_t[:]))
+        nc.vector.tensor_copy(hz_words[:], words[:].bitcast(U32).indirect(hz_t[:]))
+        offs_plane = planes[:, :S]
+        hz_plane = planes[:, S:]
+
+        def round_tile(engine_copy, raw, t, name):
+            grouped = keep.tile([P, P * PACK], BF16, name=name, align_bytes=64)
+            engine_copy(
+                grouped[:].rearrange("p (b e j) -> p b j e", e=4, j=PACK),
+                raw[:].rearrange("p j (b t e) -> p t b j e", t=TILES, e=4)[:, t],
+            )
+            return grouped
+
+        def quantise(grouped, name):
+            codes = keep.tile([P, P], U32, name=name + "_codes", align_bytes=64)
+            plane = keep.tile([P, P], U8, name=name + "_plane", align_bytes=64)
+            nc.vector.quantize_mx(out=codes[:].bitcast(FP8X4), scales=plane[:], in_=grouped[:])
+            return codes, plane
+
+        banks = [psum.tile([P, S], F32, name="bank%d" % t) for t in range(TILES)]
+
+        def product(t, weights, x_codes, x_plane, first):
+            nc.tensor.matmul_mx(
+                out=banks[t][:],
+                lhsT=weights[0][:].bitcast(FP8X4),
+                lhsT_scale=weights[1][:],
+                rhs=x_codes[:].bitcast(FP8X4),
+                rhs_scale=x_plane,
+                start=first,
+                stop=not first,
+            )
+
+        rounders = [nc.vector.tensor_copy, nc.scalar.copy]
+        quantised = {}
+        for raw, name in ((raw1, "w1"), (raw2, "w2")):
+            grouped = [round_tile(rounders[t % 2], raw, t, "%s_%d" % (name, t)) for t in range(TILES)]
+            for t in range(TILES):
+                quantised[name, t] = quantise(grouped[t], "%s_q%d" % (name, t))
+        for t in range(TILES):
+            product(t, quantised["w1", t], offs_words, offs_plane, True)
+            product(t, quantised["w2", t], hz_words, hz_plane, False)
+
+        out_rows = out.rearrange("(b t e) c -> t b e c", t=TILES, e=4)
+        for t in range(TILES):
+            h = keep.tile([P, S], F32, name="h%d" % t, align_bytes=64)
+            pa = keep.tile([P, W], F32, name="pa%d" % t, align_bytes=64)
+            pb = keep.tile([P, W], F32, name="pb%d" % t, align_bytes=64)
+            mag = keep.tile([P, W], F32, name="mag%d" % t, align_bytes=64)
+            root = keep.tile([P, W], F32, name="root%d" % t, align_bytes=64)
+            inv = keep.tile([P, W], F32, name="inv%d" % t, align_bytes=64)
+            rb = keep.tile([P, W], F32, name="rb%d" % t, align_bytes=64)
+            res = keep.tile([P, S], F32, name="res%d" % t, align_bytes=64)
+            nc.scalar.copy(h[:], banks[t][:])
+            nc.scalar.activation(pb[:], h[:].indirect(n2_t[:]), ACT.Copy)
+            if t == 0:
+                nc.vector.tensor_copy(pa[:], h[:].indirect(n1_t[:]))
+            else:
+                nc.scalar.activation(pa[:], h[:].indirect(n1_t[:]), ACT.Copy)
+            nc.scalar.activation(mag[:], pb[:], ACT.Abs)
+            nc.scalar.activation(root[:], mag[:], ACT.Abs_reciprocal_sqrt, bias=half[:])
+            nc.scalar.activation(inv[:], root[:], ACT.Square)
+            nc.vector.tensor_tensor(rb[:], pa[:], pb[:], ALU.max)
+            nc.vector.tensor_copy(res[:].indirect(n2_t[:]), rb[:])
+            nc.vector.tensor_tensor(res[:].indirect(n1_t[:]), pa[:], inv[:], ALU.mult)
+            nc.sync.dma_start(out_rows[t], res[:])

@@ -43,6 +43,8 @@ def tile_picked_othratio_none_p_kernel(tc, x_words, x_scales, w1, w2, offs, hz, 
 
         nc.gpsimd.memset(planes[:].bitcast(I32), 0)
         nc.gpsimd.memset(half[:], 0.5)
+        warm = keep.tile([P, 1], F32, name="warm")
+        nc.scalar.activation(warm[:], half[:], ACT.Abs_reciprocal_sqrt)
 
         nc.sync.dma_start(hz_t[:], hz)
         nc.sync.dma_start(offs_t[:], offs)

@@ -46,10 +46,10 @@ def tile_picked_othratio_none_p_kernel(tc, x_words, x_scales, w1, w2, offs, hz, 
         warm = keep.tile([P, 1], F32, name="warm")
         nc.scalar.activation(warm[:], half[:], ACT.Abs_reciprocal_sqrt)
 
-        nc.sync.dma_start(hz_t[:], hz)
-        nc.sync.dma_start(offs_t[:], offs)
         scale_rows = x_scales[0].bitcast(I32)
         nc.sync.dma_start(scales[:].bitcast(I32), scale_rows.unsqueeze(1).to_broadcast([16, 8, T // 4]))
+        nc.sync.dma_start(offs_t[:], offs)
+        nc.sync.dma_start(hz_t[:], hz)
         nc.sync.dma_start(n1_t[:], n1)
         nc.sync.dma_start(words[:], x_words[0].rearrange("p c r -> p (c r)").bitcast(I32))
         nc.sync.dma_start(raw1[:], w1.rearrange("(p j) m -> p j m", j=PACK))
@@ -62,8 +62,6 @@ def tile_picked_othratio_none_p_kernel(tc, x_words, x_scales, w1, w2, offs, hz, 
             nc.scalar.dma_start(planes[:].bitcast(I32)[i:P:32, :], picked_bytes[:].bitcast(I32)[8 * i : P : 32, :])
         nc.vector.tensor_copy(offs_words[:], words[:].bitcast(U32).indirect(offs_t[:]))
         nc.vector.tensor_copy(hz_words[:], words[:].bitcast(U32).indirect(hz_t[:]))
-        offs_plane = planes[:, :S]
-        hz_plane = planes[:, S:]
 
         def round_tile(engine_copy, raw, t, name):
             grouped = keep.tile([P, P * PACK], BF16, name=name, align_bytes=64)
@@ -79,49 +77,70 @@ def tile_picked_othratio_none_p_kernel(tc, x_words, x_scales, w1, w2, offs, hz, 
             nc.vector.quantize_mx(out=codes[:].bitcast(FP8X4), scales=plane[:], in_=grouped[:])
             return codes, plane
 
-        banks = [psum.tile([P, S], F32, name="bank%d" % t) for t in range(TILES)]
+        def product(bank, cols, t):
+            for name, x_codes, first in (("w1", offs_words, True), ("w2", hz_words, False)):
+                base = 0 if first else S
+                nc.tensor.matmul_mx(
+                    out=bank,
+                    lhsT=quantised[name, t][0][:].bitcast(FP8X4),
+                    lhsT_scale=quantised[name, t][1][:],
+                    rhs=x_codes[:, cols].bitcast(FP8X4),
+                    rhs_scale=planes[:, base + cols.start : base + cols.stop],
+                    start=first,
+                    stop=not first,
+                )
 
-        def product(t, weights, x_codes, x_plane, first):
-            nc.tensor.matmul_mx(
-                out=banks[t][:],
-                lhsT=weights[0][:].bitcast(FP8X4),
-                lhsT_scale=weights[1][:],
-                rhs=x_codes[:].bitcast(FP8X4),
-                rhs_scale=x_plane,
-                start=first,
-                stop=not first,
-            )
-
-        rounders = [nc.vector.tensor_copy, nc.scalar.copy]
+        on_vector = (("w1", 3), ("w2", 0), ("w2", 1))
         quantised = {}
         for raw, name in ((raw1, "w1"), (raw2, "w2")):
-            grouped = [round_tile(rounders[t % 2], raw, t, "%s_%d" % (name, t)) for t in range(TILES)]
+            grouped = []
+            for t in range(TILES):
+                engine_copy = nc.vector.tensor_copy if (name, t) in on_vector else nc.scalar.copy
+                grouped.append(round_tile(engine_copy, raw, t, "%s_%d" % (name, t)))
             for t in range(TILES):
                 quantised[name, t] = quantise(grouped[t], "%s_q%d" % (name, t))
-        for t in range(TILES):
-            product(t, quantised["w1", t], offs_words, offs_plane, True)
-            product(t, quantised["w2", t], hz_words, hz_plane, False)
 
+        def tiles(name, width):
+            return [keep.tile([P, width], F32, name="%s%d" % (name, t), align_bytes=64) for t in range(TILES)]
+
+        h = tiles("h", S)
+        res = [keep.tile([P, S], F32, name="res%d" % t, align_bytes=64) for t in range(2)]
+        pa, pb, mag, root, inv, rb = (tiles(name, W) for name in ("pa", "pb", "mag", "root", "inv", "rb"))
         out_rows = out.rearrange("(b t e) c -> t b e c", t=TILES, e=4)
+
+        low = psum.tile([P, S], F32, name="low", tag="bank_a")
+        high = psum.tile([P, S], F32, name="high", tag="bank_b")
+        product(low[:, :W], slice(0, W), 0)
+        product(high[:, :W], slice(W, S), 0)
+        nc.vector.tensor_copy(h[0][:, :W], low[:, :W])
+        nc.scalar.copy(h[0][:, W:], high[:, :W])
+        nc.vector.tensor_copy(pa[0][:], h[0][:].indirect(n1_t[:]))
+        nc.scalar.activation(pb[0][:], h[0][:].indirect(n2_t[:]), ACT.Copy)
+        nc.vector.tensor_tensor(rb[0][:], pa[0][:], pb[0][:], ALU.max)
+        nc.vector.tensor_copy(res[0][:].indirect(n2_t[:]), rb[0][:])
+
         for t in range(TILES):
-            h = keep.tile([P, S], F32, name="h%d" % t, align_bytes=64)
-            pa = keep.tile([P, W], F32, name="pa%d" % t, align_bytes=64)
-            pb = keep.tile([P, W], F32, name="pb%d" % t, align_bytes=64)
-            mag = keep.tile([P, W], F32, name="mag%d" % t, align_bytes=64)
-            root = keep.tile([P, W], F32, name="root%d" % t, align_bytes=64)
-            inv = keep.tile([P, W], F32, name="inv%d" % t, align_bytes=64)
-            rb = keep.tile([P, W], F32, name="rb%d" % t, align_bytes=64)
-            res = keep.tile([P, S], F32, name="res%d" % t, align_bytes=64)
-            nc.scalar.copy(h[:], banks[t][:])
-            nc.scalar.activation(pb[:], h[:].indirect(n2_t[:]), ACT.Copy)
+            u = t + 1
+            ahead = u < TILES
+            if ahead:
+                bank = psum.tile([P, S], F32, name="bank%d" % u, tag=("bank_a", "bank_b")[t % 2])
+                product(bank[:], slice(0, S), u)
+                nc.scalar.copy(h[u][:], bank[:])
+            nc.scalar.activation(mag[t][:], pb[t][:], ACT.Abs)
+            if ahead:
+                nc.scalar.activation(pb[u][:], h[u][:].indirect(n2_t[:]), ACT.Copy)
+            nc.scalar.activation(root[t][:], mag[t][:], ACT.Abs_reciprocal_sqrt, bias=half[:])
+            if ahead:
+                nc.scalar.activation(pa[u][:], h[u][:].indirect(n1_t[:]), ACT.Copy)
+            nc.scalar.activation(inv[t][:], root[t][:], ACT.Square)
+            if ahead:
+                nc.vector.tensor_tensor(rb[u][:], pa[u][:], pb[u][:], ALU.max)
+            if t == 2:
+                res.append(keep.tile([P, S], F32, name="res2", tag="h3", align_bytes=64))
+                res.append(keep.tile([P, S], F32, name="res3", align_bytes=64))
+                nc.vector.tensor_copy(res[2][:].indirect(n2_t[:]), rb[2][:])
+                nc.vector.tensor_copy(res[3][:].indirect(n2_t[:]), rb[3][:])
+            nc.vector.tensor_tensor(res[t][:].indirect(n1_t[:]), pa[t][:], inv[t][:], ALU.mult)
+            nc.sync.dma_start(out_rows[t], res[t][:])
             if t == 0:
-                nc.vector.tensor_copy(pa[:], h[:].indirect(n1_t[:]))
-            else:
-                nc.scalar.activation(pa[:], h[:].indirect(n1_t[:]), ACT.Copy)
-            nc.scalar.activation(mag[:], pb[:], ACT.Abs)
-            nc.scalar.activation(root[:], mag[:], ACT.Abs_reciprocal_sqrt, bias=half[:])
-            nc.scalar.activation(inv[:], root[:], ACT.Square)
-            nc.vector.tensor_tensor(rb[:], pa[:], pb[:], ALU.max)
-            nc.vector.tensor_copy(res[:].indirect(n2_t[:]), rb[:])
-            nc.vector.tensor_tensor(res[:].indirect(n1_t[:]), pa[:], inv[:], ALU.mult)
-            nc.sync.dma_start(out_rows[t], res[:])
+                nc.vector.tensor_copy(res[u][:].indirect(n2_t[:]), rb[u][:])

@@ -63,12 +63,13 @@ def tile_picked_othratio_none_p_kernel(tc, x_words, x_scales, w1, w2, offs, hz, 
         nc.vector.tensor_copy(offs_words[:], words[:].bitcast(U32).indirect(offs_t[:]))
         nc.vector.tensor_copy(hz_words[:], words[:].bitcast(U32).indirect(hz_t[:]))
 
-        def round_tile(engine_copy, raw, t, name):
+        def round_tile(shares, raw, t, name):
             grouped = keep.tile([P, P * PACK], BF16, name=name, align_bytes=64)
-            engine_copy(
-                grouped[:].rearrange("p (b e j) -> p b j e", e=4, j=PACK),
-                raw[:].rearrange("p j (b t e) -> p t b j e", t=TILES, e=4)[:, t],
-            )
+            for engine_copy, quads in shares:
+                engine_copy(
+                    grouped[:].rearrange("p (b e j) -> p b j e", e=4, j=PACK)[:, quads],
+                    raw[:].rearrange("p j (b t e) -> p t b j e", t=TILES, e=4)[:, t, quads],
+                )
             return grouped
 
         def quantise(grouped, name):
@@ -96,7 +97,10 @@ def tile_picked_othratio_none_p_kernel(tc, x_words, x_scales, w1, w2, offs, hz, 
             grouped = []
             for t in range(TILES):
                 engine_copy = nc.vector.tensor_copy if (name, t) in on_vector else nc.scalar.copy
-                grouped.append(round_tile(engine_copy, raw, t, "%s_%d" % (name, t)))
+                shares = ((engine_copy, slice(0, 32)),)
+                if (name, t) == ("w2", 0):
+                    shares = ((nc.scalar.copy, slice(0, 14)), (nc.vector.tensor_copy, slice(14, 32)))
+                grouped.append(round_tile(shares, raw, t, "%s_%d" % (name, t)))
             for t in range(TILES):
                 quantised[name, t] = quantise(grouped[t], "%s_q%d" % (name, t))
 
@@ -129,8 +133,10 @@ def tile_picked_othratio_none_p_kernel(tc, x_words, x_scales, w1, w2, offs, hz, 
             nc.scalar.activation(mag[t][:], pb[t][:], ACT.Abs)
             if ahead:
                 nc.scalar.activation(pb[u][:], h[u][:].indirect(n2_t[:]), ACT.Copy)
+            if t == 2:
+                nc.scalar.activation(pa[u][:], h[u][:].indirect(n1_t[:]), ACT.Copy)
             nc.scalar.activation(root[t][:], mag[t][:], ACT.Abs_reciprocal_sqrt, bias=half[:])
-            if ahead:
+            if t < 2:
                 nc.scalar.activation(pa[u][:], h[u][:].indirect(n1_t[:]), ACT.Copy)
             nc.scalar.activation(inv[t][:], root[t][:], ACT.Square)
             if ahead:

from contextlib import ExitStack

import concourse.mybir as mybir

K, T, S, N, W = 512, 2048, 512, 512, 256
FLOPS = 2 * 2 * K * S * N

F32 = mybir.dt.float32
BF16 = mybir.dt.bfloat16
I32 = mybir.dt.int32
U32 = mybir.dt.uint32
U16 = mybir.dt.uint16
U8 = mybir.dt.uint8
FP8X4 = mybir.dt.float8_e4m3fn_x4
ACT = mybir.ActivationFunctionType
ALU = mybir.AluOpType

P = 128
PACK = 4
TILES = N // P


def tile_picked_othratio_none_p_kernel(tc, x_words, x_scales, w1, w2, offs, hz, n1, n2, out):
    nc = tc.nc
    with ExitStack() as ctx:
        keep = ctx.enter_context(tc.tile_pool(name="keep", bufs=1))
        psum = ctx.enter_context(tc.psum_pool(name="psum", bufs=1))

        words = keep.tile([P, T], I32, name="words", align_bytes=64)
        scales = keep.tile([P, T], U8, name="scales", align_bytes=64)
        offs_t = keep.tile([P, S // 16], U16, name="offs_t")
        hz_t = keep.tile([P, S // 16], U16, name="hz_t")
        n1_t = keep.tile([P, W // 16], U16, name="n1_t")
        n2_t = keep.tile([P, W // 16], U16, name="n2_t")
        raw1 = keep.tile([P, PACK, N], F32, name="raw1", align_bytes=64)
        raw2 = keep.tile([P, PACK, N], F32, name="raw2", align_bytes=64)
        half = keep.tile([P, 1], F32, name="half")

        picked_bytes = keep.tile([P, 2 * S], U8, name="picked_bytes", align_bytes=64)
        planes = keep.tile([P, 2 * S], U8, name="planes", align_bytes=64)
        offs_words = keep.tile([P, S], U32, name="offs_words", align_bytes=64)
        hz_words = keep.tile([P, S], U32, name="hz_words", align_bytes=64)

        nc.gpsimd.memset(planes[:].bitcast(I32), 0)
        nc.gpsimd.memset(half[:], 0.5)
        warm = keep.tile([P, 1], F32, name="warm")
        nc.scalar.activation(warm[:], half[:], ACT.Abs_reciprocal_sqrt)

        scale_rows = x_scales[0].bitcast(I32)
        nc.sync.dma_start(scales[:].bitcast(I32), scale_rows.unsqueeze(1).to_broadcast([16, 8, T // 4]))
        nc.sync.dma_start(offs_t[:], offs)
        nc.sync.dma_start(hz_t[:], hz)
        nc.sync.dma_start(n1_t[:], n1)
        nc.sync.dma_start(words[:], x_words[0].rearrange("p c r -> p (c r)").bitcast(I32))
        nc.sync.dma_start(raw1[:], w1.rearrange("(p j) m -> p j m", j=PACK))
        nc.sync.dma_start(raw2[:], w2.rearrange("(p j) m -> p j m", j=PACK))
        nc.sync.dma_start(n2_t[:], n2)

        nc.vector.tensor_copy(picked_bytes[:, :S], scales[:].indirect(offs_t[:]))
        nc.vector.tensor_copy(picked_bytes[:, S:], scales[:].indirect(hz_t[:]))
        for i in range(4):
            nc.scalar.dma_start(planes[:].bitcast(I32)[i:P:32, :], picked_bytes[:].bitcast(I32)[8 * i : P : 32, :])
        nc.vector.tensor_copy(offs_words[:], words[:].bitcast(U32).indirect(offs_t[:]))
        nc.vector.tensor_copy(hz_words[:], words[:].bitcast(U32).indirect(hz_t[:]))

        def round_tile(shares, raw, t, name):
            grouped = keep.tile([P, P * PACK], BF16, name=name, align_bytes=64)
            for engine_copy, quads in shares:
                engine_copy(
                    grouped[:].rearrange("p (b e j) -> p b j e", e=4, j=PACK)[:, quads],
                    raw[:].rearrange("p j (b t e) -> p t b j e", t=TILES, e=4)[:, t, quads],
                )
            return grouped

        def quantise(grouped, name):
            codes = keep.tile([P, P], U32, name=name + "_codes", align_bytes=64)
            plane = keep.tile([P, P], U8, name=name + "_plane", align_bytes=64)
            nc.vector.quantize_mx(out=codes[:].bitcast(FP8X4), scales=plane[:], in_=grouped[:])
            return codes, plane

        def product(bank, cols, t):
            for name, x_codes, first in (("w1", offs_words, True), ("w2", hz_words, False)):
                base = 0 if first else S
                nc.tensor.matmul_mx(
                    out=bank,
                    lhsT=quantised[name, t][0][:].bitcast(FP8X4),
                    lhsT_scale=quantised[name, t][1][:],
                    rhs=x_codes[:, cols].bitcast(FP8X4),
                    rhs_scale=planes[:, base + cols.start : base + cols.stop],
                    start=first,
                    stop=not first,
                )

        on_vector = (("w1", 3), ("w2", 0), ("w2", 1))
        quantised = {}
        for raw, name in ((raw1, "w1"), (raw2, "w2")):
            grouped = []
            for t in range(TILES):
                engine_copy = nc.vector.tensor_copy if (name, t) in on_vector else nc.scalar.copy
                shares = ((engine_copy, slice(0, 32)),)
                if (name, t) == ("w2", 0):
                    shares = ((nc.scalar.copy, slice(0, 14)), (nc.vector.tensor_copy, slice(14, 32)))
                grouped.append(round_tile(shares, raw, t, "%s_%d" % (name, t)))
            for t in range(TILES):
                quantised[name, t] = quantise(grouped[t], "%s_q%d" % (name, t))

        def tiles(name, width):
            return [keep.tile([P, width], F32, name="%s%d" % (name, t), align_bytes=64) for t in range(TILES)]

        h = tiles("h", S)
        res = [keep.tile([P, S], F32, name="res%d" % t, align_bytes=64) for t in range(2)]
        pa, pb, mag, root, inv, rb = (tiles(name, W) for name in ("pa", "pb", "mag", "root", "inv", "rb"))
        out_rows = out.rearrange("(b t e) c -> t b e c", t=TILES, e=4)

        low = psum.tile([P, S], F32, name="low", tag="bank_a")
        high = psum.tile([P, S], F32, name="high", tag="bank_b")
        product(low[:, :W], slice(0, W), 0)
        product(high[:, :W], slice(W, S), 0)
        nc.vector.tensor_copy(h[0][:, :W], low[:, :W])
        nc.scalar.copy(h[0][:, W:], high[:, :W])
        nc.vector.tensor_copy(pa[0][:], h[0][:].indirect(n1_t[:]))
        nc.scalar.activation(pb[0][:], h[0][:].indirect(n2_t[:]), ACT.Copy)
        nc.vector.tensor_tensor(rb[0][:], pa[0][:], pb[0][:], ALU.max)
        nc.vector.tensor_copy(res[0][:].indirect(n2_t[:]), rb[0][:])

        for t in range(TILES):
            u = t + 1
            ahead = u < TILES
            if ahead:
                bank = psum.tile([P, S], F32, name="bank%d" % u, tag=("bank_a", "bank_b")[t % 2])
                product(bank[:], slice(0, S), u)
                nc.scalar.copy(h[u][:], bank[:])
            nc.scalar.activation(mag[t][:], pb[t][:], ACT.Abs)
            if ahead:
                nc.scalar.activation(pb[u][:], h[u][:].indirect(n2_t[:]), ACT.Copy)
            if t == 2:
                nc.scalar.activation(pa[u][:], h[u][:].indirect(n1_t[:]), ACT.Copy)
            nc.scalar.activation(root[t][:], mag[t][:], ACT.Abs_reciprocal_sqrt, bias=half[:])
            if t < 2:
                nc.scalar.activation(pa[u][:], h[u][:].indirect(n1_t[:]), ACT.Copy)
            nc.scalar.activation(inv[t][:], root[t][:], ACT.Square)
            if ahead:
                nc.vector.tensor_tensor(rb[u][:], pa[u][:], pb[u][:], ALU.max)
            if t == 2:
                res.append(keep.tile([P, S], F32, name="res2", tag="h3", align_bytes=64))
                res.append(keep.tile([P, S], F32, name="res3", align_bytes=64))
                nc.vector.tensor_copy(res[2][:].indirect(n2_t[:]), rb[2][:])
                nc.vector.tensor_copy(res[3][:].indirect(n2_t[:]), rb[3][:])
            nc.vector.tensor_tensor(res[t][:].indirect(n1_t[:]), pa[t][:], inv[t][:], ALU.mult)
            nc.sync.dma_start(out_rows[t], res[t][:])
            if t == 0:
                nc.vector.tensor_copy(res[u][:].indirect(n2_t[:]), rb[u][:])
